import numpy as np
import ml_dtypes


def mxq(x, axis, fmt="e4m3"):
    dtype, down = {"e4m3": (ml_dtypes.float8_e4m3fn, 7), "e5m2": (ml_dtypes.float8_e5m2, 14)}[fmt]
    v = np.moveaxis(np.asarray(x, np.float32).astype(ml_dtypes.bfloat16).astype(np.float64), axis, -1)
    blocks = v.reshape(v.shape[:-1] + (-1, 32))
    amax = np.abs(blocks).max(-1, keepdims=True)
    byte = np.maximum(np.where(amax > 0, np.frexp(amax)[1] - 1 + 127, 0) - down, 1)
    scale = np.exp2(byte - 127.0)
    codes = (blocks / scale).astype(np.float32).astype(dtype).astype(np.float64)
    return np.moveaxis((codes * scale).reshape(v.shape), -1, axis)


WIDE = False


def mx_kscale(k):
    if not WIDE:
        return np.ones(k)
    levels = np.array([10, -10, 5, -5, 0])
    if k % 512:
        return np.exp2(np.random.permutation(np.resize(levels, k // 32))).repeat(32)
    a = np.empty((k // 512, 16))
    for p in range(k // 512):
        a[p, :8] = np.random.permutation(np.resize(levels, 8))
        for g in range(8):
            far = levels[np.abs(levels - a[p, g]) >= 10]
            a[p, g + 8] = far[np.random.randint(len(far))]
    return np.exp2(a.ravel()).repeat(32)


def f64(x):
    return np.asarray(x).astype(np.float64)


def striped(idx):
    return np.tile(idx.reshape(-1, 16).T, (8, 1)).astype(np.uint16)


def unstriped(offs):
    return offs[:16].T.reshape(-1).astype(np.int64)


def striped8(idx):
    return np.concatenate([x.reshape(-1, 16).T for x in idx]).astype(np.uint16)


def runs(offs, k):
    lists = np.stack([offs[16 * r : 16 * r + 16].T.reshape(-1) for r in range(8)]).astype(np.int64)
    return lists[np.arange(k) % 512 // 64]


def pack_weight(w):
    k, n = w.shape
    w = f64(np.asarray(w, np.float32).astype(ml_dtypes.bfloat16)).reshape(k // 32, 32, n)
    amax = np.abs(w).max(1)
    byte = np.clip(np.where(amax > 0, np.frexp(amax)[1] - 1 + 127 - 7, 1), 1, 254)
    scaled = (w * np.exp2(127.0 - byte)[:, None, :]).reshape(k, n).astype(np.float32)
    words = np.ascontiguousarray(scaled.reshape(k // 512, 128, 4, n).transpose(0, 1, 3, 2)).astype(ml_dtypes.float8_e4m3fn).view(np.uint8)
    return words, np.ascontiguousarray(byte.astype(np.uint8).reshape(k // 512, 16, n))


def unpack_weight(words, scales):
    g, p, n, _ = words.shape
    vals = np.ascontiguousarray(words).view(ml_dtypes.float8_e4m3fn).astype(np.float64) * np.repeat(np.exp2(scales.astype(np.float64) - 127.0), 8, axis=1)[..., None]
    return vals.transpose(0, 1, 3, 2).reshape(g * 512, n)


E2M1 = np.array([0.0, 0.5, 1.0, 1.5, 2.0, 3.0, 4.0, 6.0, -0.0, -0.5, -1.0, -1.5, -2.0, -3.0, -4.0, -6.0])


def pack_fp4(w):
    k, n = w.shape
    w = f64(np.asarray(w, np.float32).astype(ml_dtypes.bfloat16)).reshape(k // 32, 32, n)
    amax = np.abs(w).max(1)
    mant, ex = np.frexp(amax / 6.0)
    byte = np.clip(np.where(amax > 0, np.where(mant > 0.5, ex, ex - 1) + 127, 1), 1, 254)
    scaled = (w * np.exp2(127.0 - byte)[:, None, :]).reshape(k, n).astype(np.float32)
    c = np.ascontiguousarray(scaled.reshape(k // 512, 128, 4, n).transpose(0, 1, 3, 2)).astype(ml_dtypes.float4_e2m1fn).view(np.uint8) & 0xF
    words = (c[..., 0::2] | (c[..., 1::2] << 4)).reshape(k // 512, 128, 2 * n)
    return np.ascontiguousarray(words), np.ascontiguousarray(byte.astype(np.uint8).reshape(k // 512, 16, n))


def unpack_fp4(words, scales):
    g, _, n = scales.shape
    words = np.ascontiguousarray(words).reshape(g, 128, n, 2)
    nib = np.empty((g, 128, n, 4), np.uint8)
    nib[..., 0::2] = words & 0xF
    nib[..., 1::2] = words >> 4
    vals = E2M1[nib] * np.repeat(np.exp2(scales.astype(np.float64) - 127.0), 8, axis=1)[..., None]
    return vals.transpose(0, 1, 3, 2).reshape(g * 512, n)


def planes(y):
    n, m = y.shape
    v = y.astype(np.float32).astype(ml_dtypes.bfloat16).astype(np.float64).reshape(n // 32, 32, m)
    top = np.abs(v).max(1)
    byte = np.clip(np.where(top > 0, np.frexp(top)[1] - 1 + 127 - 7, 1), 1, 254)
    codes = (v * np.exp2(127.0 - byte)[:, None, :]).reshape(n, m).astype(np.float32).astype(ml_dtypes.float8_e4m3fn).view(np.uint8)
    words = codes.reshape(n // 512, 128, 4, m).transpose(0, 1, 3, 2)
    return np.ascontiguousarray(words), np.ascontiguousarray(byte.astype(np.uint8).reshape(n // 512, 16, m))


K, T, S, N, H, W = 512, 2048, 512, 512, 512, 2048


def setup_inputs():
    n = np.random.standard_normal
    s = mx_kscale(K)[:, None]
    u = mx_kscale(H)
    packed_xT = pack_weight(n((K, T)) * s)
    packed_w1 = pack_fp4(n((K, H)) / np.sqrt(K) / s)
    packed_w2 = pack_fp4(n((H, N)) / np.sqrt(2 * H) / u[:, None])
    packed_w3 = pack_fp4(n((K, N)) / np.sqrt(2 * K) / s)
    return {
        "x_words": packed_xT[0],
        "x_scales": packed_xT[1],
        "w1_words": packed_w1[0],
        "w1_scales": packed_w1[1],
        "gn": (np.random.uniform(0.5, 1.5, (H, 1)) * u[:, None]).astype(np.float32),
        "w2_words": packed_w2[0],
        "w2_scales": packed_w2[1],
        "w3_words": packed_w3[0],
        "w3_scales": packed_w3[1],
        "offs": striped(np.random.permutation(T)[:S]),
        "n1": striped8(np.stack([np.random.permutation(S) for _ in range(8)])),
        "n2": striped8(np.stack([np.random.permutation(S) for _ in range(8)])),
        "hz": striped8(np.random.randint(0, T, (8, S))),
        "n3": striped(np.random.randint(0, S, W)),
    }


def reference(x_words, x_scales, w1_words, w1_scales, gn, w2_words, w2_scales, w3_words, w3_scales, offs, n1, n2, hz, n3):
    xq = unpack_weight(x_words, x_scales)[:, unstriped(offs)]
    y = unpack_fp4(w1_words, w1_scales).T @ xq
    z = f64(gn) * ((y[np.arange(H)[:, None], runs(n1, H)]) * (y[np.arange(H)[:, None], runs(n2, H)]))
    x_hz = unpack_weight(x_words, x_scales)[np.arange(K)[:, None], runs(hz, K)]
    h = unpack_fp4(w2_words, w2_scales).T @ mxq(z, 0, "e4m3") + unpack_fp4(w3_words, w3_scales).T @ x_hz
    mb = h[:, unstriped(n3)]
    mx = mb.reshape(N, S, 4).max(axis=2)
    mn = mb.reshape(N, S, 4).min(axis=2)
    out_0 = mx - (0.5 * mn)
    return (out_0,) + planes(out_0)

@@ -1,0 +1,242 @@
+from contextlib import ExitStack
+
+import concourse.mybir as mybir
+
+K, T, S, N, H, W = 512, 2048, 512, 512, 512, 2048
+FLOPS = 3 * 2 * 512 * 512 * 512
+
+F32 = mybir.dt.float32
+BF16 = mybir.dt.bfloat16
+I32 = mybir.dt.int32
+U32 = mybir.dt.uint32
+U16 = mybir.dt.uint16
+U8 = mybir.dt.uint8
+FP8X4 = mybir.dt.float8_e4m3fn_x4
+FP4X4 = mybir.dt.float4_e2m1fn_x4
+ALU = mybir.AluOpType
+COPY = mybir.ActivationFunctionType.Copy
+
+P = 128
+PACK = 4
+QUADS = 4
+MEMBERS = 4
+Z_PARTS = ((0, 256), (256, 128), (384, 128))
+OUT_CHUNKS = ((0, 128), (128, 128), (256, 128), (384, 128))
+H_SPARE = 32
+ODD_RUN_AT = 14
+
+
+def tile_picked_mixhprodgspan_none_po_kernel(
+    tc, x_words, x_scales, w1_words, w1_scales, gn, w2_words, w2_scales, w3_words, w3_scales,
+    offs, n1, n2, hz, n3, out_0, out_1, out_2,
+):
+    nc = tc.nc
+    with ExitStack() as ctx:
+        keep = ctx.enter_context(tc.tile_pool(name="keep", bufs=1))
+        psum = ctx.enter_context(tc.psum_pool(name="psum", bufs=1))
+
+        def sb(name, shape, dtype):
+            return keep.tile(shape, dtype, name=name, align_bytes=64)
+
+        def entries(lst, start, count):
+            return lst[:, start // 16 : (start + count) // 16]
+
+        def load_scale_rows(queue, tile, rows, first):
+            for q in range(QUADS):
+                queue.dma_start(
+                    tile[32 * q + first : 32 * q + first + 4, :].bitcast(I32),
+                    rows[0, 4 * q : 4 * q + 4, :].bitcast(I32),
+                )
+
+        def interleave(dst, src):
+            nc.vector.tensor_copy(
+                dst[:].rearrange("p (c i) t -> p c t i", i=4),
+                src[:].rearrange("p t (c i) -> p c t i", i=4),
+            )
+
+        xw = sb("xw", [P, T], I32)
+        xs = sb("xs", [P, T], U8)
+        xs_hz = sb("xs_hz", [P, T], U8)
+        w_raw = [sb(f"w_raw{i}", [P, 2 * N], U8) for i in range(3)]
+        ws_raw = [sb(f"ws_raw{i}", [P, N], U8) for i in range(3)]
+        w_deal = [sb(f"w_deal{i}", [P, 2 * N], U8) for i in range(3)]
+        ws_deal = [sb(f"ws_deal{i}", [P, N], U8) for i in range(3)]
+        hz_scales = sb("hz_scales", [P, S], U8)
+        h_win = [sb(f"h_win{t}", [P, S + H_SPARE], F32) for t in range(PACK)]
+        offs_t = keep.tile([P, S // 16], U16, name="offs_t")
+        n1_t = keep.tile([P, S // 16], U16, name="n1_t")
+        n2_t = keep.tile([P, S // 16], U16, name="n2_t")
+        hz_t = keep.tile([P, S // 16], U16, name="hz_t")
+        n3_t = keep.tile([P, W // 16], U16, name="n3_t")
+        gain = sb("gain", [P, PACK], F32)
+
+        nc.vector.memset(xs[:].bitcast(I32), 0)
+        nc.gpsimd.memset(ws_raw[0][:].bitcast(I32), 0)
+        nc.gpsimd.memset(xs_hz[:].bitcast(I32), 0)
+        nc.gpsimd.memset(ws_raw[1][:].bitcast(I32), 0)
+        nc.gpsimd.memset(ws_raw[2][:].bitcast(I32), 0)
+        nc.gpsimd.memset(hz_scales[:].bitcast(I32), 0)
+        for t in range(PACK):
+            nc.gpsimd.memset(h_win[t][:, S:], 0.0)
+
+        nc.sync.dma_start(xw[:], x_words[0].rearrange("p c r -> p (c r)").bitcast(I32))
+        nc.sync.dma_start(offs_t[:], offs)
+        nc.sync.dma_start(w_raw[0][:].bitcast(I32), w1_words[0].bitcast(I32))
+        load_scale_rows(nc.scalar, xs, x_scales, 0)
+        load_scale_rows(nc.scalar, ws_raw[0], w1_scales, 0)
+        nc.sync.dma_start(hz_t[:], hz)
+        load_scale_rows(nc.scalar, xs_hz, x_scales, ODD_RUN_AT)
+        nc.sync.dma_start(w_raw[2][:].bitcast(I32), w3_words[0].bitcast(I32))
+        nc.sync.dma_start(w_raw[1][:].bitcast(I32), w2_words[0].bitcast(I32))
+        nc.sync.dma_start(n1_t[:], n1)
+        nc.sync.dma_start(n2_t[:], n2)
+        nc.sync.dma_start(gain[:], gn.rearrange("(p t) o -> p (t o)", t=PACK))
+        load_scale_rows(nc.sync, ws_raw[2], w3_scales, 0)
+        load_scale_rows(nc.sync, ws_raw[1], w2_scales, 0)
+        nc.sync.dma_start(n3_t[:], n3)
+
+        def deal_words(i):
+            nc.vector.tensor_copy(
+                w_deal[i][:].rearrange("p (t m b) -> p t m b", t=PACK, b=2),
+                w_raw[i][:].rearrange("p (m t b) -> p t m b", t=PACK, b=2),
+            )
+
+        def deal_scales(i):
+            nc.vector.tensor_copy(
+                ws_deal[i][:].rearrange("p (t m) -> p t m", t=PACK),
+                ws_raw[i][:].rearrange("p (m t) -> p t m", t=PACK),
+            )
+
+        def product(out, i, t, words, scales, start, stop):
+            nc.tensor.matmul_mx(
+                out=out,
+                lhsT=w_deal[i][:, 2 * P * t : 2 * P * (t + 1)].bitcast(FP4X4),
+                lhsT_scale=ws_deal[i][:, P * t : P * (t + 1)],
+                rhs=words.bitcast(FP8X4),
+                rhs_scale=scales,
+                start=start,
+                stop=stop,
+            )
+
+        xq_words = sb("xq_words", [P, S], U32)
+        xq_scales = sb("xq_scales", [P, S], U8)
+        hz_words = sb("hz_words", [P, S], U32)
+        hz_picked = sb("hz_picked", [P, S], U8)
+        deal_words(0)
+        nc.vector.tensor_copy(xq_scales[:], xs[:].indirect(offs_t[:]))
+        deal_scales(0)
+        nc.vector.tensor_copy(xq_words[:], xw[:].bitcast(U32).indirect(offs_t[:]))
+        nc.vector.tensor_copy(hz_picked[:], xs_hz[:].indirect(hz_t[:]))
+        nc.vector.tensor_copy(hz_words[:], xw[:].bitcast(U32).indirect(hz_t[:]))
+        for q in range(QUADS):
+            nc.sync.dma_start(
+                hz_scales[32 * q : 32 * q + 4, :].bitcast(I32),
+                hz_picked[32 * q + ODD_RUN_AT : 32 * q + ODD_RUN_AT + 4, :].bitcast(I32),
+            )
+        for i in (2, 1):
+            deal_words(i)
+            deal_scales(i)
+
+        y_bank = [psum.tile([P, S], F32, name=f"bank{t}") for t in range(PACK)]
+        y_win = [sb(f"y_win{t}", [P, S], F32) for t in range(PACK)]
+        for t in range(PACK):
+            product(y_bank[t][:], 0, t, xq_words[:], xq_scales[:], True, True)
+
+        first = [sb(f"first{a}", [P, PACK, w], F32) for a, (j0, w) in enumerate(Z_PARTS)]
+        second = [sb(f"second{a}", [P, PACK, w], F32) for a, (j0, w) in enumerate(Z_PARTS)]
+        z_planes = [sb(f"z_planes{a}", [P, PACK, w], BF16) for a, (j0, w) in enumerate(Z_PARTS)]
+        z_packed = [sb(f"z_packed{a}", [P, w, PACK], BF16) for a, (j0, w) in enumerate(Z_PARTS)]
+        z_words = [sb(f"z_words{a}", [P, w], U32) for a, (j0, w) in enumerate(Z_PARTS)]
+        z_scales = [sb(f"z_scales{a}", [P, w], U8) for a, (j0, w) in enumerate(Z_PARTS)]
+        last = len(Z_PARTS) - 1
+
+        def fetch(a):
+            j0, w = Z_PARTS[a]
+            for t in range(PACK):
+                if a == 0:
+                    nc.scalar.copy(y_win[t][:], y_bank[t][:])
+                nc.scalar.activation(first[a][:, t, :], y_win[t][:].indirect(entries(n1_t, j0, w)), COPY)
+                looked_up = y_win[t][:].indirect(entries(n2_t, j0, w))
+                if t == PACK - 1 and a < last:
+                    nc.scalar.activation(second[a][:, t, :], looked_up, COPY)
+                else:
+                    nc.vector.tensor_copy(second[a][:, t, :], looked_up)
+
+        def multiply(a):
+            for t in range(PACK):
+                nc.vector.scalar_tensor_tensor(
+                    z_planes[a][:, t, :], first[a][:, t, :], gain[:, t : t + 1], second[a][:, t, :], ALU.mult, ALU.mult
+                )
+            interleave(z_packed[a], z_planes[a])
+
+        def quantise(a):
+            nc.vector.quantize_mx(
+                out=z_words[a][:].bitcast(FP8X4), scales=z_scales[a][:], in_=z_packed[a][:].rearrange("p w t -> p (w t)")
+            )
+
+        h_bank = {}
+
+        def h_products(a):
+            j0, w = Z_PARTS[a]
+            per_bank = 1 if a == last else S // w
+            for t0 in range(0, PACK, per_bank):
+                name = f"bank{t0}" if a == last else f"h_bank{a}_{t0}"
+                bank = psum.tile([P, per_bank, w], F32, name=name)
+                for u in range(per_bank):
+                    h_bank[a, t0 + u] = bank[:, u, :]
+            for t in range(PACK):
+                product(h_bank[a, t], 2, t, hz_words[:, j0 : j0 + w], hz_scales[:, j0 : j0 + w], True, False)
+                product(h_bank[a, t], 1, t, z_words[a][:], z_scales[a][:], False, True)
+
+        fetch(0)
+        for a in range(len(Z_PARTS)):
+            multiply(a)
+            if a < last:
+                fetch(a + 1)
+            quantise(a)
+            h_products(a)
+
+        for a, (j0, w) in enumerate(Z_PARTS):
+            for t in range(PACK):
+                if a < last or t == 0:
+                    nc.scalar.copy(h_win[t][:, j0 : j0 + w], h_bank[a, t])
+                else:
+                    nc.vector.tensor_copy(h_win[t][:, j0 : j0 + w], h_bank[a, t])
+
+        out_rows = out_0.rearrange("(p t) j -> p t j", t=PACK)
+        out_words = out_1[0].rearrange("p c r -> p (c r)").bitcast(I32)
+        o_scales = sb("o_scales", [P, S], U8)
+        for c, (j0, w) in enumerate(OUT_CHUNKS):
+            members = sb(f"members{c}", [P, PACK, MEMBERS * w], F32)
+            pair_max = sb(f"pair_max{c}", [P, PACK, w, 2], F32)
+            pair_min = sb(f"pair_min{c}", [P, PACK, w, 2], F32)
+            largest = sb(f"largest{c}", [P, PACK, w], F32)
+            smallest = sb(f"smallest{c}", [P, PACK, w], F32)
+            span = sb(f"span{c}", [P, PACK, w], F32)
+            o_packed = sb(f"o_packed{c}", [P, w, PACK], BF16)
+            o_words = sb(f"o_words{c}", [P, w], U32)
+            for t in range(PACK):
+                nc.scalar.activation(
+                    members[:, t, :], h_win[t][:].indirect(entries(n3_t, MEMBERS * j0, MEMBERS * w)), COPY
+                )
+            groups = members[:].rearrange("p t (j m) -> p t j m", m=MEMBERS)
+            for t0 in range(0, PACK, 2):
+                ts = slice(t0, t0 + 2)
+                nc.vector.tensor_tensor(pair_max[:, ts], groups[:, ts, :, 0:2], groups[:, ts, :, 2:4], ALU.max)
+                nc.vector.tensor_tensor(pair_min[:, ts], groups[:, ts, :, 0:2], groups[:, ts, :, 2:4], ALU.min)
+                nc.vector.tensor_tensor(largest[:, ts], pair_max[:, ts, :, 0], pair_max[:, ts, :, 1], ALU.max)
+                nc.vector.tensor_tensor(smallest[:, ts], pair_min[:, ts, :, 0], pair_min[:, ts, :, 1], ALU.min)
+                nc.vector.scalar_tensor_tensor(span[:, ts], smallest[:, ts], -0.5, largest[:, ts], ALU.mult, ALU.add)
+            nc.sync.dma_start(out_rows[:, :, j0 : j0 + w], span[:])
+            interleave(o_packed, span)
+            nc.vector.quantize_mx(
+                out=o_words[:].bitcast(FP8X4),
+                scales=o_scales[:, j0 : j0 + w],
+                in_=o_packed[:].rearrange("p w t -> p (w t)"),
+            )
+            nc.sync.dma_start(out_words[:, j0 : j0 + w], o_words[:].bitcast(I32))
+        for q in range(QUADS):
+            queue = nc.scalar if q % 2 == 0 else nc.sync
+            queue.dma_start(
+                out_2[0, 4 * q : 4 * q + 4, :].bitcast(I32), o_scales[32 * q : 32 * q + 4, :].bitcast(I32)
+            )

@@ -23,7 +23,7 @@ MEMBERS = 4
 Z_PARTS = ((0, 256), (256, 128), (384, 128))
 OUT_CHUNKS = ((0, 128), (128, 128), (256, 128), (384, 128))
 H_SPARE = 32
-ODD_RUN_AT = 14
+ODD_RUN_AT = 16
 
 
 def tile_picked_mixhprodgspan_none_po_kernel(
@@ -48,6 +48,13 @@ def tile_picked_mixhprodgspan_none_po_kernel(
                     rows[0, 4 * q : 4 * q + 4, :].bitcast(I32),
                 )
 
+        def fill_scale_rows(queue, tile, rows, quads):
+            for q in quads:
+                queue.dma_start(
+                    tile[32 * q : 32 * q + 32, :].bitcast(I32),
+                    rows[0, 4 * q : 4 * q + 4, :].bitcast(I32).partition_broadcast(8),
+                )
+
         def interleave(dst, src):
             nc.vector.tensor_copy(
                 dst[:].rearrange("p (c i) t -> p c t i", i=4),
@@ -56,7 +63,6 @@ def tile_picked_mixhprodgspan_none_po_kernel(
 
         xw = sb("xw", [P, T], I32)
         xs = sb("xs", [P, T], U8)
-        xs_hz = sb("xs_hz", [P, T], U8)
         w_raw = [sb(f"w_raw{i}", [P, 2 * N], U8) for i in range(3)]
         ws_raw = [sb(f"ws_raw{i}", [P, N], U8) for i in range(3)]
         w_deal = [sb(f"w_deal{i}", [P, 2 * N], U8) for i in range(3)]
@@ -70,28 +76,25 @@ def tile_picked_mixhprodgspan_none_po_kernel(
         n3_t = keep.tile([P, W // 16], U16, name="n3_t")
         gain = sb("gain", [P, PACK], F32)
 
-        nc.vector.memset(xs[:].bitcast(I32), 0)
-        nc.gpsimd.memset(ws_raw[0][:].bitcast(I32), 0)
-        nc.gpsimd.memset(xs_hz[:].bitcast(I32), 0)
-        nc.gpsimd.memset(ws_raw[1][:].bitcast(I32), 0)
-        nc.gpsimd.memset(ws_raw[2][:].bitcast(I32), 0)
         nc.gpsimd.memset(hz_scales[:].bitcast(I32), 0)
         for t in range(PACK):
             nc.gpsimd.memset(h_win[t][:, S:], 0.0)
+        nc.gpsimd.memset(ws_raw[2][:].bitcast(I32), 0)
+        nc.gpsimd.memset(ws_raw[1][:].bitcast(I32), 0)
 
-        nc.sync.dma_start(xw[:], x_words[0].rearrange("p c r -> p (c r)").bitcast(I32))
         nc.sync.dma_start(offs_t[:], offs)
+        fill_scale_rows(nc.sync, xs, x_scales, range(1))
         nc.sync.dma_start(w_raw[0][:].bitcast(I32), w1_words[0].bitcast(I32))
-        load_scale_rows(nc.scalar, xs, x_scales, 0)
-        load_scale_rows(nc.scalar, ws_raw[0], w1_scales, 0)
-        nc.sync.dma_start(hz_t[:], hz)
-        load_scale_rows(nc.scalar, xs_hz, x_scales, ODD_RUN_AT)
-        nc.sync.dma_start(w_raw[2][:].bitcast(I32), w3_words[0].bitcast(I32))
-        nc.sync.dma_start(w_raw[1][:].bitcast(I32), w2_words[0].bitcast(I32))
+        nc.sync.dma_start(xw[:], x_words[0].rearrange("p c r -> p (c r)").bitcast(I32))
+        fill_scale_rows(nc.scalar, xs, x_scales, range(1, QUADS))
+        fill_scale_rows(nc.scalar, ws_raw[0], w1_scales, range(QUADS))
         nc.sync.dma_start(n1_t[:], n1)
         nc.sync.dma_start(n2_t[:], n2)
-        nc.sync.dma_start(gain[:], gn.rearrange("(p t) o -> p (t o)", t=PACK))
+        nc.sync.dma_start(w_raw[2][:].bitcast(I32), w3_words[0].bitcast(I32))
+        nc.sync.dma_start(hz_t[:], hz)
+        nc.sync.dma_start(w_raw[1][:].bitcast(I32), w2_words[0].bitcast(I32))
         load_scale_rows(nc.sync, ws_raw[2], w3_scales, 0)
+        nc.sync.dma_start(gain[:], gn.rearrange("(p t) o -> p (t o)", t=PACK))
         load_scale_rows(nc.sync, ws_raw[1], w2_scales, 0)
         nc.sync.dma_start(n3_t[:], n3)
 
@@ -124,15 +127,13 @@ def tile_picked_mixhprodgspan_none_po_kernel(
         hz_picked = sb("hz_picked", [P, S], U8)
         deal_words(0)
         nc.vector.tensor_copy(xq_scales[:], xs[:].indirect(offs_t[:]))
-        deal_scales(0)
         nc.vector.tensor_copy(xq_words[:], xw[:].bitcast(U32).indirect(offs_t[:]))
-        nc.vector.tensor_copy(hz_picked[:], xs_hz[:].indirect(hz_t[:]))
+        deal_scales(0)
+        nc.vector.tensor_copy(hz_picked[:], xs[:].indirect(hz_t[:]))
         nc.vector.tensor_copy(hz_words[:], xw[:].bitcast(U32).indirect(hz_t[:]))
-        for q in range(QUADS):
-            nc.sync.dma_start(
-                hz_scales[32 * q : 32 * q + 4, :].bitcast(I32),
-                hz_picked[32 * q + ODD_RUN_AT : 32 * q + ODD_RUN_AT + 4, :].bitcast(I32),
-            )
+        for r in range(4):
+            at = r if r < 2 else ODD_RUN_AT + r
+            nc.sync.dma_start(hz_scales[r:P:32, :].bitcast(I32), hz_picked[at:P:32, :].bitcast(I32))
         for i in (2, 1):
             deal_words(i)
             deal_scales(i)
@@ -157,84 +158,123 @@ def tile_picked_mixhprodgspan_none_po_kernel(
                     nc.scalar.copy(y_win[t][:], y_bank[t][:])
                 nc.scalar.activation(first[a][:, t, :], y_win[t][:].indirect(entries(n1_t, j0, w)), COPY)
                 looked_up = y_win[t][:].indirect(entries(n2_t, j0, w))
-                if t == PACK - 1 and a < last:
+                if a > 0 or t == PACK - 1:
                     nc.scalar.activation(second[a][:, t, :], looked_up, COPY)
                 else:
                     nc.vector.tensor_copy(second[a][:, t, :], looked_up)
 
-        def multiply(a):
-            for t in range(PACK):
-                nc.vector.scalar_tensor_tensor(
-                    z_planes[a][:, t, :], first[a][:, t, :], gain[:, t : t + 1], second[a][:, t, :], ALU.mult, ALU.mult
-                )
-            interleave(z_packed[a], z_planes[a])
+        def multiply(a, t):
+            nc.vector.scalar_tensor_tensor(
+                z_planes[a][:, t, :], first[a][:, t, :], gain[:, t : t + 1], second[a][:, t, :], ALU.mult, ALU.mult
+            )
 
         def quantise(a):
             nc.vector.quantize_mx(
                 out=z_words[a][:].bitcast(FP8X4), scales=z_scales[a][:], in_=z_packed[a][:].rearrange("p w t -> p (w t)")
             )
 
-        h_bank = {}
+        early = Z_PARTS[last][0]
+        h_early = [psum.tile([P, early], F32, name=f"h_early{t}") for t in range(PACK)]
+        h_late = [psum.tile([P, S - early], F32, name=f"bank{t}") for t in range(PACK)]
+
+        def h_part(a, t):
+            j0, w = Z_PARTS[a]
+            return h_late[t][:] if a == last else h_early[t][:, j0 : j0 + w]
 
         def h_products(a):
-            j0, w = Z_PARTS[a]
-            per_bank = 1 if a == last else S // w
-            for t0 in range(0, PACK, per_bank):
-                name = f"bank{t0}" if a == last else f"h_bank{a}_{t0}"
-                bank = psum.tile([P, per_bank, w], F32, name=name)
-                for u in range(per_bank):
-                    h_bank[a, t0 + u] = bank[:, u, :]
             for t in range(PACK):
-                product(h_bank[a, t], 2, t, hz_words[:, j0 : j0 + w], hz_scales[:, j0 : j0 + w], True, False)
-                product(h_bank[a, t], 1, t, z_words[a][:], z_scales[a][:], False, True)
+                product(h_part(a, t), 1, t, z_words[a][:], z_scales[a][:], False, a >= last - 1)
 
-        fetch(0)
         for a in range(len(Z_PARTS)):
-            multiply(a)
-            if a < last:
-                fetch(a + 1)
-            quantise(a)
-            h_products(a)
-
+            fetch(a)
         for a, (j0, w) in enumerate(Z_PARTS):
             for t in range(PACK):
-                if a < last or t == 0:
-                    nc.scalar.copy(h_win[t][:, j0 : j0 + w], h_bank[a, t])
-                else:
-                    nc.vector.tensor_copy(h_win[t][:, j0 : j0 + w], h_bank[a, t])
+                product(h_part(a, t), 2, t, hz_words[:, j0 : j0 + w], hz_scales[:, j0 : j0 + w], a in (0, last), False)
+        for a in range(len(Z_PARTS) + 1):
+            if a <= last:
+                multiply(a, 0)
+            if a > 0:
+                interleave(z_packed[a - 1], z_planes[a - 1])
+            if a <= last:
+                multiply(a, 1)
+            if a > 0:
+                quantise(a - 1)
+                h_products(a - 1)
+            if a <= last:
+                multiply(a, 2)
+                multiply(a, 3)
+
+        for t in range(PACK):
+            nc.scalar.copy(h_win[t][:, :early], h_early[t][:])
+        nc.scalar.copy(h_win[0][:, early:S], h_late[0][:])
+        for t in range(1, PACK):
+            nc.vector.tensor_copy(h_win[t][:, early:S], h_late[t][:])
 
         out_rows = out_0.rearrange("(p t) j -> p t j", t=PACK)
         out_words = out_1[0].rearrange("p c r -> p (c r)").bitcast(I32)
         o_scales = sb("o_scales", [P, S], U8)
+        def chunk_tiles(name, tail, dtype):
+            return [sb(f"{name}{c}", [P] + tail(w), dtype) for c, (j0, w) in enumerate(OUT_CHUNKS)]
+
+        members = chunk_tiles("members", lambda w: [PACK, w, MEMBERS], F32)
+        pair_max = chunk_tiles("pair_max", lambda w: [PACK, w, 2], F32)
+        pair_min = chunk_tiles("pair_min", lambda w: [PACK, w, 2], F32)
+        largest = chunk_tiles("largest", lambda w: [PACK, w], F32)
+        smallest = chunk_tiles("smallest", lambda w: [PACK, w], F32)
+        span = chunk_tiles("span", lambda w: [PACK, w], F32)
+        o_packed = chunk_tiles("o_packed", lambda w: [w, PACK], BF16)
+        o_words = chunk_tiles("o_words", lambda w: [w], U32)
+
         for c, (j0, w) in enumerate(OUT_CHUNKS):
-            members = sb(f"members{c}", [P, PACK, MEMBERS * w], F32)
-            pair_max = sb(f"pair_max{c}", [P, PACK, w, 2], F32)
-            pair_min = sb(f"pair_min{c}", [P, PACK, w, 2], F32)
-            largest = sb(f"largest{c}", [P, PACK, w], F32)
-            smallest = sb(f"smallest{c}", [P, PACK, w], F32)
-            span = sb(f"span{c}", [P, PACK, w], F32)
-            o_packed = sb(f"o_packed{c}", [P, w, PACK], BF16)
-            o_words = sb(f"o_words{c}", [P, w], U32)
             for t in range(PACK):
                 nc.scalar.activation(
-                    members[:, t, :], h_win[t][:].indirect(entries(n3_t, MEMBERS * j0, MEMBERS * w)), COPY
+                    members[c][:, t].rearrange("p j m -> p (j m)"),
+                    h_win[t][:].indirect(entries(n3_t, MEMBERS * j0, MEMBERS * w)),
+                    COPY,
                 )
-            groups = members[:].rearrange("p t (j m) -> p t j m", m=MEMBERS)
-            for t0 in range(0, PACK, 2):
-                ts = slice(t0, t0 + 2)
-                nc.vector.tensor_tensor(pair_max[:, ts], groups[:, ts, :, 0:2], groups[:, ts, :, 2:4], ALU.max)
-                nc.vector.tensor_tensor(pair_min[:, ts], groups[:, ts, :, 0:2], groups[:, ts, :, 2:4], ALU.min)
-                nc.vector.tensor_tensor(largest[:, ts], pair_max[:, ts, :, 0], pair_max[:, ts, :, 1], ALU.max)
-                nc.vector.tensor_tensor(smallest[:, ts], pair_min[:, ts, :, 0], pair_min[:, ts, :, 1], ALU.min)
-                nc.vector.scalar_tensor_tensor(span[:, ts], smallest[:, ts], -0.5, largest[:, ts], ALU.mult, ALU.add)
-            nc.sync.dma_start(out_rows[:, :, j0 : j0 + w], span[:])
-            interleave(o_packed, span)
-            nc.vector.quantize_mx(
-                out=o_words[:].bitcast(FP8X4),
-                scales=o_scales[:, j0 : j0 + w],
-                in_=o_packed[:].rearrange("p w t -> p (w t)"),
+
+        def pairs(dst, c, ts, op):
+            nc.vector.tensor_tensor(dst[c][:, ts], members[c][:, ts, :, 0:2], members[c][:, ts, :, 2:4], op)
+
+        def fours(dst, src, c, ts, op):
+            nc.vector.tensor_tensor(dst[c][:, ts], src[c][:, ts, :, 0], src[c][:, ts, :, 1], op)
+
+        def combine(c, ts):
+            nc.vector.scalar_tensor_tensor(
+                span[c][:, ts], smallest[c][:, ts], -0.5, largest[c][:, ts], ALU.mult, ALU.add
             )
-            nc.sync.dma_start(out_words[:, j0 : j0 + w], o_words[:].bitcast(I32))
+            if ts.stop == PACK:
+                j0, w = OUT_CHUNKS[c]
+                nc.sync.dma_start(out_rows[:, :, j0 : j0 + w], span[c][:])
+
+        def planes(c):
+            j0, w = OUT_CHUNKS[c]
+            nc.vector.quantize_mx(
+                out=o_words[c][:].bitcast(FP8X4),
+                scales=o_scales[:, j0 : j0 + w],
+                in_=o_packed[c][:].rearrange("p w t -> p (w t)"),
+            )
+            nc.sync.dma_start(out_words[:, j0 : j0 + w], o_words[c][:].bitcast(I32))
+
+        singles, doubles = [(t, t + 1) for t in range(PACK)], [(0, 2), (2, 4)]
+        cuts = [singles, doubles, doubles, doubles[:1] + singles[2:]]
+        steps = [(c, slice(*cut)) for c in range(len(OUT_CHUNKS)) for cut in cuts[c]]
+        for now, before in zip(steps + [None], [None] + steps):
+            closes = before is not None and before[1].stop == PACK
+            if now:
+                pairs(pair_max, *now, ALU.max)
+            if before:
+                combine(*before)
+            if now:
+                pairs(pair_min, *now, ALU.min)
+            if closes:
+                interleave(o_packed[before[0]], span[before[0]])
+            if now:
+                fours(largest, pair_max, *now, ALU.max)
+            if closes:
+                planes(before[0])
+            if now:
+                fours(smallest, pair_min, *now, ALU.min)
         for q in range(QUADS):
             queue = nc.scalar if q % 2 == 0 else nc.sync
             queue.dma_start(

@@ -23,7 +23,7 @@ MEMBERS = 4
 Z_PARTS = ((0, 256), (256, 128), (384, 128))
 OUT_CHUNKS = ((0, 128), (128, 128), (256, 128), (384, 128))
 H_SPARE = 32
-ODD_RUN_AT = 16
+ROW_STEP = 8
 
 
 def tile_picked_mixhprodgspan_none_po_kernel(
@@ -41,19 +41,23 @@ def tile_picked_mixhprodgspan_none_po_kernel(
         def entries(lst, start, count):
             return lst[:, start // 16 : (start + count) // 16]
 
-        def load_scale_rows(queue, tile, rows, first):
+        def load_scale_rows(queues, tile, rows):
+            for q, queue in enumerate(queues):
+                queue.dma_start(tile[32 * q : 32 * q + 4, :].bitcast(I32), rows[0, 4 * q : 4 * q + 4, :].bitcast(I32))
+
+        def place_scale_rows(queue, plane, picked):
             for q in range(QUADS):
                 queue.dma_start(
-                    tile[32 * q + first : 32 * q + first + 4, :].bitcast(I32),
-                    rows[0, 4 * q : 4 * q + 4, :].bitcast(I32),
+                    plane[32 * q : 32 * q + 4, :].bitcast(I32),
+                    picked[32 * q : 32 * q + 32 : ROW_STEP, :].bitcast(I32),
                 )
 
-        def fill_scale_rows(queue, tile, rows, quads):
-            for q in quads:
-                queue.dma_start(
-                    tile[32 * q : 32 * q + 32, :].bitcast(I32),
-                    rows[0, 4 * q : 4 * q + 4, :].bitcast(I32).partition_broadcast(8),
-                )
+        def spread_scale_rows(queue, tile, rows):
+            queue.dma_start(tile[0:P:ROW_STEP].bitcast(I32), rows[0].bitcast(I32))
+
+        def close_up_scale_rows(queue, tile):
+            for r in range(1, 4):
+                queue.dma_start(tile[r:P:32].bitcast(I32), tile[ROW_STEP * r : P : 32].bitcast(I32))
 
         def interleave(dst, src):
             nc.vector.tensor_copy(
@@ -63,10 +67,16 @@ def tile_picked_mixhprodgspan_none_po_kernel(
 
         xw = sb("xw", [P, T], I32)
         xs = sb("xs", [P, T], U8)
-        w_raw = [sb(f"w_raw{i}", [P, 2 * N], U8) for i in range(3)]
-        ws_raw = [sb(f"ws_raw{i}", [P, N], U8) for i in range(3)]
+        w1_raw = sb("w1_raw", [P, 2 * N], U8)
+        w23_raw = sb("w23_raw", [P, 4 * N], U8)
+        w_raw = [w1_raw[:], w23_raw[:, : 2 * N], w23_raw[:, 2 * N :]]
+        xs_hz = sb("xs_hz", [P, T], U8)
+        ws1_raw = w23_raw[:, 3 * N // 2 : 5 * N // 2]
+        ws1_deal = sb("ws1_deal", [P, N], U8)
+        ws23_raw = sb("ws23_raw", [P, 2 * N], U8)
+        ws23_deal = sb("ws23_deal", [P, 2 * N], U8)
         w_deal = [sb(f"w_deal{i}", [P, 2 * N], U8) for i in range(3)]
-        ws_deal = [sb(f"ws_deal{i}", [P, N], U8) for i in range(3)]
+        ws_deal = [ws1_deal[:], ws23_deal[:, :N], ws23_deal[:, N:]]
         hz_scales = sb("hz_scales", [P, S], U8)
         h_win = [sb(f"h_win{t}", [P, S + H_SPARE], F32) for t in range(PACK)]
         offs_t = keep.tile([P, S // 16], U16, name="offs_t")
@@ -76,38 +86,38 @@ def tile_picked_mixhprodgspan_none_po_kernel(
         n3_t = keep.tile([P, W // 16], U16, name="n3_t")
         gain = sb("gain", [P, PACK], F32)
 
+        nc.vector.memset(xs[:].bitcast(I32), 0)
+        nc.vector.memset(ws1_raw[:].bitcast(I32), 0)
+        nc.vector.memset(xs_hz[:].bitcast(I32), 0)
+        nc.vector.memset(ws23_raw[:].bitcast(I32), 0)
+
+        nc.sync.dma_start(offs_t[:], offs)
+        nc.sync.dma_start(w_raw[0].bitcast(I32), w1_words[0].bitcast(I32))
+        nc.sync.dma_start(n1_t[:], n1)
+        nc.sync.dma_start(n2_t[:], n2)
+        nc.sync.dma_start(hz_t[:], hz)
+        nc.sync.dma_start(n3_t[:], n3)
+        nc.sync.dma_start(gain[:], gn.rearrange("(p t) o -> p (t o)", t=PACK))
+        nc.sync.dma_start(xw[:], x_words[0].rearrange("p c r -> p (c r)").bitcast(I32))
+        load_scale_rows([nc.scalar] * QUADS, xs, x_scales)
+        load_scale_rows([nc.scalar] * QUADS, ws1_raw, w1_scales)
+        spread_scale_rows(nc.scalar, xs_hz[:], x_scales)
+        spread_scale_rows(nc.scalar, ws23_raw[:, N:], w3_scales)
+        spread_scale_rows(nc.scalar, ws23_raw[:, :N], w2_scales)
         nc.gpsimd.memset(hz_scales[:].bitcast(I32), 0)
         for t in range(PACK):
             nc.gpsimd.memset(h_win[t][:, S:], 0.0)
-        nc.gpsimd.memset(ws_raw[2][:].bitcast(I32), 0)
-        nc.gpsimd.memset(ws_raw[1][:].bitcast(I32), 0)
-
-        nc.sync.dma_start(offs_t[:], offs)
-        fill_scale_rows(nc.sync, xs, x_scales, range(1))
-        nc.sync.dma_start(w_raw[0][:].bitcast(I32), w1_words[0].bitcast(I32))
-        nc.sync.dma_start(xw[:], x_words[0].rearrange("p c r -> p (c r)").bitcast(I32))
-        fill_scale_rows(nc.scalar, xs, x_scales, range(1, QUADS))
-        fill_scale_rows(nc.scalar, ws_raw[0], w1_scales, range(QUADS))
-        nc.sync.dma_start(n1_t[:], n1)
-        nc.sync.dma_start(n2_t[:], n2)
-        nc.sync.dma_start(w_raw[2][:].bitcast(I32), w3_words[0].bitcast(I32))
-        nc.sync.dma_start(hz_t[:], hz)
-        nc.sync.dma_start(w_raw[1][:].bitcast(I32), w2_words[0].bitcast(I32))
-        load_scale_rows(nc.sync, ws_raw[2], w3_scales, 0)
-        nc.sync.dma_start(gain[:], gn.rearrange("(p t) o -> p (t o)", t=PACK))
-        load_scale_rows(nc.sync, ws_raw[1], w2_scales, 0)
-        nc.sync.dma_start(n3_t[:], n3)
 
         def deal_words(i):
             nc.vector.tensor_copy(
                 w_deal[i][:].rearrange("p (t m b) -> p t m b", t=PACK, b=2),
-                w_raw[i][:].rearrange("p (m t b) -> p t m b", t=PACK, b=2),
+                w_raw[i].rearrange("p (m t b) -> p t m b", t=PACK, b=2),
             )
 
-        def deal_scales(i):
+        def deal_scales(dealt, raw):
             nc.vector.tensor_copy(
-                ws_deal[i][:].rearrange("p (t m) -> p t m", t=PACK),
-                ws_raw[i][:].rearrange("p (m t) -> p t m", t=PACK),
+                dealt[:].rearrange("p (i t m) -> p i t m", t=PACK, m=P),
+                raw[:].rearrange("p (i m t) -> p i t m", t=PACK, m=P),
             )
 
         def product(out, i, t, words, scales, start, stop):
@@ -121,27 +131,28 @@ def tile_picked_mixhprodgspan_none_po_kernel(
                 stop=stop,
             )
 
-        xq_words = sb("xq_words", [P, S], U32)
-        xq_scales = sb("xq_scales", [P, S], U8)
-        hz_words = sb("hz_words", [P, S], U32)
-        hz_picked = sb("hz_picked", [P, S], U8)
+        picked_words = sb("picked_words", [P, S], U32)
+        picked_scales = sb("picked_scales", [P, S], U8)
         deal_words(0)
-        nc.vector.tensor_copy(xq_scales[:], xs[:].indirect(offs_t[:]))
-        nc.vector.tensor_copy(xq_words[:], xw[:].bitcast(U32).indirect(offs_t[:]))
-        deal_scales(0)
-        nc.vector.tensor_copy(hz_picked[:], xs[:].indirect(hz_t[:]))
-        nc.vector.tensor_copy(hz_words[:], xw[:].bitcast(U32).indirect(hz_t[:]))
-        for r in range(4):
-            at = r if r < 2 else ODD_RUN_AT + r
-            nc.sync.dma_start(hz_scales[r:P:32, :].bitcast(I32), hz_picked[at:P:32, :].bitcast(I32))
-        for i in (2, 1):
-            deal_words(i)
-            deal_scales(i)
+        deal_scales(ws1_deal, ws1_raw)
+        nc.sync.dma_start(w_raw[2].bitcast(I32), w3_words[0].bitcast(I32))
+        nc.sync.dma_start(w_raw[1].bitcast(I32), w2_words[0].bitcast(I32))
+        nc.vector.tensor_copy(picked_scales[:], xs[:].indirect(offs_t[:]))
+        nc.vector.tensor_copy(picked_words[:], xw[:].bitcast(U32).indirect(offs_t[:]))
 
         y_bank = [psum.tile([P, S], F32, name=f"bank{t}") for t in range(PACK)]
         y_win = [sb(f"y_win{t}", [P, S], F32) for t in range(PACK)]
         for t in range(PACK):
-            product(y_bank[t][:], 0, t, xq_words[:], xq_scales[:], True, True)
+            product(y_bank[t][:], 0, t, picked_words[:], picked_scales[:], True, True)
+
+        hz_picked = sb("hz_picked", [P, S], U8)
+        nc.vector.tensor_copy(hz_picked[:], xs_hz[:].indirect(hz_t[:]))
+        place_scale_rows(nc.sync, hz_scales, hz_picked)
+        deal_scales(ws23_deal, ws23_raw)
+        close_up_scale_rows(nc.sync, ws23_deal)
+        nc.vector.tensor_copy(picked_words[:], xw[:].bitcast(U32).indirect(hz_t[:]))
+        deal_words(2)
+        deal_words(1)
 
         first = [sb(f"first{a}", [P, PACK, w], F32) for a, (j0, w) in enumerate(Z_PARTS)]
         second = [sb(f"second{a}", [P, PACK, w], F32) for a, (j0, w) in enumerate(Z_PARTS)]
@@ -158,7 +169,7 @@ def tile_picked_mixhprodgspan_none_po_kernel(
                     nc.scalar.copy(y_win[t][:], y_bank[t][:])
                 nc.scalar.activation(first[a][:, t, :], y_win[t][:].indirect(entries(n1_t, j0, w)), COPY)
                 looked_up = y_win[t][:].indirect(entries(n2_t, j0, w))
-                if a > 0 or t == PACK - 1:
+                if a > 0 and (a, t) != (1, 0):
                     nc.scalar.activation(second[a][:, t, :], looked_up, COPY)
                 else:
                     nc.vector.tensor_copy(second[a][:, t, :], looked_up)
@@ -189,7 +200,7 @@ def tile_picked_mixhprodgspan_none_po_kernel(
             fetch(a)
         for a, (j0, w) in enumerate(Z_PARTS):
             for t in range(PACK):
-                product(h_part(a, t), 2, t, hz_words[:, j0 : j0 + w], hz_scales[:, j0 : j0 + w], a in (0, last), False)
+                product(h_part(a, t), 2, t, picked_words[:, j0 : j0 + w], hz_scales[:, j0 : j0 + w], a in (0, last), False)
         for a in range(len(Z_PARTS) + 1):
             if a <= last:
                 multiply(a, 0)
@@ -204,10 +215,12 @@ def tile_picked_mixhprodgspan_none_po_kernel(
                 multiply(a, 2)
                 multiply(a, 3)
 
-        for t in range(PACK):
+        for t in range(PACK - 1):
             nc.scalar.copy(h_win[t][:, :early], h_early[t][:])
         nc.scalar.copy(h_win[0][:, early:S], h_late[0][:])
         for t in range(1, PACK):
+            if t == PACK - 1:
+                nc.vector.tensor_copy(h_win[t][:, :early], h_early[t][:])
             nc.vector.tensor_copy(h_win[t][:, early:S], h_late[t][:])
 
         out_rows = out_0.rearrange("(p t) j -> p t j", t=PACK)
@@ -257,7 +270,7 @@ def tile_picked_mixhprodgspan_none_po_kernel(
             nc.sync.dma_start(out_words[:, j0 : j0 + w], o_words[c][:].bitcast(I32))
 
         singles, doubles = [(t, t + 1) for t in range(PACK)], [(0, 2), (2, 4)]
-        cuts = [singles, doubles, doubles, doubles[:1] + singles[2:]]
+        cuts = [singles, doubles, doubles, doubles]
         steps = [(c, slice(*cut)) for c in range(len(OUT_CHUNKS)) for cut in cuts[c]]
         for now, before in zip(steps + [None], [None] + steps):
             closes = before is not None and before[1].stop == PACK

@@ -59,8 +59,8 @@ def tile_picked_mixhprodgspan_none_po_kernel(
             for r in range(1, 4):
                 queue.dma_start(tile[r:P:32].bitcast(I32), tile[ROW_STEP * r : P : 32].bitcast(I32))
 
-        def interleave(dst, src):
-            nc.vector.tensor_copy(
+        def interleave(copy, dst, src):
+            copy(
                 dst[:].rearrange("p (c i) t -> p c t i", i=4),
                 src[:].rearrange("p t (c i) -> p c t i", i=4),
             )
@@ -86,24 +86,24 @@ def tile_picked_mixhprodgspan_none_po_kernel(
         n3_t = keep.tile([P, W // 16], U16, name="n3_t")
         gain = sb("gain", [P, PACK], F32)
 
+        nc.gpsimd.memset(ws1_raw.bitcast(I32), 0)
         nc.vector.memset(xs[:].bitcast(I32), 0)
-        nc.vector.memset(ws1_raw[:].bitcast(I32), 0)
-        nc.vector.memset(xs_hz[:].bitcast(I32), 0)
+        nc.gpsimd.memset(xs_hz[:].bitcast(I32), 0)
         nc.vector.memset(ws23_raw[:].bitcast(I32), 0)
 
         nc.sync.dma_start(offs_t[:], offs)
         nc.sync.dma_start(w_raw[0].bitcast(I32), w1_words[0].bitcast(I32))
+        load_scale_rows([nc.sync] * QUADS, ws1_raw, w1_scales)
         nc.sync.dma_start(n1_t[:], n1)
+        nc.sync.dma_start(xw[:], x_words[0].rearrange("p c r -> p (c r)").bitcast(I32))
+        load_scale_rows([nc.sync] * QUADS, xs, x_scales)
+        spread_scale_rows(nc.sync, xs_hz[:], x_scales)
+        spread_scale_rows(nc.sync, ws23_raw[:, N:], w3_scales)
+        spread_scale_rows(nc.sync, ws23_raw[:, :N], w2_scales)
         nc.sync.dma_start(n2_t[:], n2)
         nc.sync.dma_start(hz_t[:], hz)
-        nc.sync.dma_start(n3_t[:], n3)
         nc.sync.dma_start(gain[:], gn.rearrange("(p t) o -> p (t o)", t=PACK))
-        nc.sync.dma_start(xw[:], x_words[0].rearrange("p c r -> p (c r)").bitcast(I32))
-        load_scale_rows([nc.scalar] * QUADS, xs, x_scales)
-        load_scale_rows([nc.scalar] * QUADS, ws1_raw, w1_scales)
-        spread_scale_rows(nc.scalar, xs_hz[:], x_scales)
-        spread_scale_rows(nc.scalar, ws23_raw[:, N:], w3_scales)
-        spread_scale_rows(nc.scalar, ws23_raw[:, :N], w2_scales)
+        nc.sync.dma_start(n3_t[:], n3)
         nc.gpsimd.memset(hz_scales[:].bitcast(I32), 0)
         for t in range(PACK):
             nc.gpsimd.memset(h_win[t][:, S:], 0.0)
@@ -137,19 +137,23 @@ def tile_picked_mixhprodgspan_none_po_kernel(
         deal_scales(ws1_deal, ws1_raw)
         nc.sync.dma_start(w_raw[2].bitcast(I32), w3_words[0].bitcast(I32))
         nc.sync.dma_start(w_raw[1].bitcast(I32), w2_words[0].bitcast(I32))
-        nc.vector.tensor_copy(picked_scales[:], xs[:].indirect(offs_t[:]))
         nc.vector.tensor_copy(picked_words[:], xw[:].bitcast(U32).indirect(offs_t[:]))
+        halves = [slice(0, S // 2), slice(S // 2, S)]
+        for cols in halves:
+            nc.vector.tensor_copy(picked_scales[:, cols], xs[:].indirect(entries(offs_t, cols.start, S // 2)))
 
         y_bank = [psum.tile([P, S], F32, name=f"bank{t}") for t in range(PACK)]
         y_win = [sb(f"y_win{t}", [P, S], F32) for t in range(PACK)]
-        for t in range(PACK):
+        for cols in halves:
+            product(y_bank[0][:, cols], 0, 0, picked_words[:, cols], picked_scales[:, cols], True, True)
+        for t in range(1, PACK):
             product(y_bank[t][:], 0, t, picked_words[:], picked_scales[:], True, True)
 
         hz_picked = sb("hz_picked", [P, S], U8)
-        nc.vector.tensor_copy(hz_picked[:], xs_hz[:].indirect(hz_t[:]))
-        place_scale_rows(nc.sync, hz_scales, hz_picked)
         deal_scales(ws23_deal, ws23_raw)
         close_up_scale_rows(nc.sync, ws23_deal)
+        nc.vector.tensor_copy(hz_picked[:], xs_hz[:].indirect(hz_t[:]))
+        place_scale_rows(nc.sync, hz_scales, hz_picked)
         nc.vector.tensor_copy(picked_words[:], xw[:].bitcast(U32).indirect(hz_t[:]))
         deal_words(2)
         deal_words(1)
@@ -169,7 +173,7 @@ def tile_picked_mixhprodgspan_none_po_kernel(
                     nc.scalar.copy(y_win[t][:], y_bank[t][:])
                 nc.scalar.activation(first[a][:, t, :], y_win[t][:].indirect(entries(n1_t, j0, w)), COPY)
                 looked_up = y_win[t][:].indirect(entries(n2_t, j0, w))
-                if a > 0 and (a, t) != (1, 0):
+                if a > 0:
                     nc.scalar.activation(second[a][:, t, :], looked_up, COPY)
                 else:
                     nc.vector.tensor_copy(second[a][:, t, :], looked_up)
@@ -201,25 +205,18 @@ def tile_picked_mixhprodgspan_none_po_kernel(
         for a, (j0, w) in enumerate(Z_PARTS):
             for t in range(PACK):
                 product(h_part(a, t), 2, t, picked_words[:, j0 : j0 + w], hz_scales[:, j0 : j0 + w], a in (0, last), False)
-        for a in range(len(Z_PARTS) + 1):
-            if a <= last:
-                multiply(a, 0)
-            if a > 0:
-                interleave(z_packed[a - 1], z_planes[a - 1])
-            if a <= last:
-                multiply(a, 1)
-            if a > 0:
-                quantise(a - 1)
-                h_products(a - 1)
-            if a <= last:
-                multiply(a, 2)
-                multiply(a, 3)
+        for a in range(len(Z_PARTS)):
+            for t in range(PACK):
+                multiply(a, t)
+            interleave(nc.vector.tensor_copy, z_packed[a], z_planes[a])
+            quantise(a)
+            h_products(a)
 
-        for t in range(PACK - 1):
+        for t in range(2):
             nc.scalar.copy(h_win[t][:, :early], h_early[t][:])
         nc.scalar.copy(h_win[0][:, early:S], h_late[0][:])
         for t in range(1, PACK):
-            if t == PACK - 1:
+            if t >= 2:
                 nc.vector.tensor_copy(h_win[t][:, :early], h_early[t][:])
             nc.vector.tensor_copy(h_win[t][:, early:S], h_late[t][:])
 
@@ -272,6 +269,7 @@ def tile_picked_mixhprodgspan_none_po_kernel(
         singles, doubles = [(t, t + 1) for t in range(PACK)], [(0, 2), (2, 4)]
         cuts = [singles, doubles, doubles, doubles]
         steps = [(c, slice(*cut)) for c in range(len(OUT_CHUNKS)) for cut in cuts[c]]
+        late_chunk = len(OUT_CHUNKS) - 2
         for now, before in zip(steps + [None], [None] + steps):
             closes = before is not None and before[1].stop == PACK
             if now:
@@ -281,10 +279,13 @@ def tile_picked_mixhprodgspan_none_po_kernel(
             if now:
                 pairs(pair_min, *now, ALU.min)
             if closes:
-                interleave(o_packed[before[0]], span[before[0]])
+                copy = nc.scalar.copy if before[0] == late_chunk else nc.vector.tensor_copy
+                interleave(copy, o_packed[before[0]], span[before[0]])
             if now:
                 fours(largest, pair_max, *now, ALU.max)
-            if closes:
+            if closes and before[0] != late_chunk:
+                if now is None:
+                    planes(late_chunk)
                 planes(before[0])
             if now:
                 fours(smallest, pair_min, *now, ALU.min)

@@ -2,7 +2,7 @@ from contextlib import ExitStack
 
 import concourse.mybir as mybir
 
-K, T, S, N, H, W = 512, 2048, 512, 512, 512, 2048
+T, S, N, W = 2048, 512, 512, 2048
 FLOPS = 3 * 2 * 512 * 512 * 512
 
 F32 = mybir.dt.float32
@@ -24,6 +24,8 @@ Z_PARTS = ((0, 256), (256, 128), (384, 128))
 OUT_CHUNKS = ((0, 128), (128, 128), (256, 128), (384, 128))
 H_SPARE = 32
 ROW_STEP = 8
+W1, W2, W3 = 0, 1, 2
+SCALAR_BANKS = 2
 
 
 def tile_picked_mixhprodgspan_none_po_kernel(
@@ -41,26 +43,28 @@ def tile_picked_mixhprodgspan_none_po_kernel(
         def entries(lst, start, count):
             return lst[:, start // 16 : (start + count) // 16]
 
-        def load_scale_rows(queues, tile, rows):
-            for q, queue in enumerate(queues):
-                queue.dma_start(tile[32 * q : 32 * q + 4, :].bitcast(I32), rows[0, 4 * q : 4 * q + 4, :].bitcast(I32))
-
-        def place_scale_rows(queue, plane, picked):
+        def load_scale_rows(plane, rows):
             for q in range(QUADS):
-                queue.dma_start(
-                    plane[32 * q : 32 * q + 4, :].bitcast(I32),
-                    picked[32 * q : 32 * q + 32 : ROW_STEP, :].bitcast(I32),
+                nc.sync.dma_start(
+                    plane[32 * q : 32 * q + 4, :].bitcast(I32), rows[0, 4 * q : 4 * q + 4, :].bitcast(I32)
                 )
 
-        def spread_scale_rows(queue, tile, rows):
-            queue.dma_start(tile[0:P:ROW_STEP].bitcast(I32), rows[0].bitcast(I32))
+        def place_scale_rows(plane, spread):
+            for q in range(QUADS):
+                nc.sync.dma_start(
+                    plane[32 * q : 32 * q + 4, :].bitcast(I32),
+                    spread[32 * q : 32 * q + 32 : ROW_STEP, :].bitcast(I32),
+                )
 
-        def close_up_scale_rows(queue, tile):
+        def spread_scale_rows(spread, rows):
+            nc.sync.dma_start(spread[0:P:ROW_STEP].bitcast(I32), rows[0].bitcast(I32))
+
+        def close_up_scale_rows(spread):
             for r in range(1, 4):
-                queue.dma_start(tile[r:P:32].bitcast(I32), tile[ROW_STEP * r : P : 32].bitcast(I32))
+                nc.sync.dma_start(spread[r:P:32].bitcast(I32), spread[ROW_STEP * r : P : 32].bitcast(I32))
 
-        def interleave(copy, dst, src):
-            copy(
+        def interleave(dst, src):
+            nc.vector.tensor_copy(
                 dst[:].rearrange("p (c i) t -> p c t i", i=4),
                 src[:].rearrange("p t (c i) -> p c t i", i=4),
             )
@@ -92,14 +96,14 @@ def tile_picked_mixhprodgspan_none_po_kernel(
         nc.vector.memset(ws23_raw[:].bitcast(I32), 0)
 
         nc.sync.dma_start(offs_t[:], offs)
-        nc.sync.dma_start(w_raw[0].bitcast(I32), w1_words[0].bitcast(I32))
-        load_scale_rows([nc.sync] * QUADS, ws1_raw, w1_scales)
+        nc.sync.dma_start(w_raw[W1].bitcast(I32), w1_words[0].bitcast(I32))
+        load_scale_rows(ws1_raw, w1_scales)
         nc.sync.dma_start(n1_t[:], n1)
         nc.sync.dma_start(xw[:], x_words[0].rearrange("p c r -> p (c r)").bitcast(I32))
-        load_scale_rows([nc.sync] * QUADS, xs, x_scales)
-        spread_scale_rows(nc.sync, xs_hz[:], x_scales)
-        spread_scale_rows(nc.sync, ws23_raw[:, N:], w3_scales)
-        spread_scale_rows(nc.sync, ws23_raw[:, :N], w2_scales)
+        load_scale_rows(xs, x_scales)
+        spread_scale_rows(xs_hz[:], x_scales)
+        spread_scale_rows(ws23_raw[:, N:], w3_scales)
+        spread_scale_rows(ws23_raw[:, :N], w2_scales)
         nc.sync.dma_start(n2_t[:], n2)
         nc.sync.dma_start(hz_t[:], hz)
         nc.sync.dma_start(gain[:], gn.rearrange("(p t) o -> p (t o)", t=PACK))
@@ -133,10 +137,10 @@ def tile_picked_mixhprodgspan_none_po_kernel(
 
         picked_words = sb("picked_words", [P, S], U32)
         picked_scales = sb("picked_scales", [P, S], U8)
-        deal_words(0)
+        deal_words(W1)
         deal_scales(ws1_deal, ws1_raw)
-        nc.sync.dma_start(w_raw[2].bitcast(I32), w3_words[0].bitcast(I32))
-        nc.sync.dma_start(w_raw[1].bitcast(I32), w2_words[0].bitcast(I32))
+        nc.sync.dma_start(w_raw[W3].bitcast(I32), w3_words[0].bitcast(I32))
+        nc.sync.dma_start(w_raw[W2].bitcast(I32), w2_words[0].bitcast(I32))
         nc.vector.tensor_copy(picked_words[:], xw[:].bitcast(U32).indirect(offs_t[:]))
         halves = [slice(0, S // 2), slice(S // 2, S)]
         for cols in halves:
@@ -145,18 +149,18 @@ def tile_picked_mixhprodgspan_none_po_kernel(
         y_bank = [psum.tile([P, S], F32, name=f"bank{t}") for t in range(PACK)]
         y_win = [sb(f"y_win{t}", [P, S], F32) for t in range(PACK)]
         for cols in halves:
-            product(y_bank[0][:, cols], 0, 0, picked_words[:, cols], picked_scales[:, cols], True, True)
+            product(y_bank[0][:, cols], W1, 0, picked_words[:, cols], picked_scales[:, cols], True, True)
         for t in range(1, PACK):
-            product(y_bank[t][:], 0, t, picked_words[:], picked_scales[:], True, True)
+            product(y_bank[t][:], W1, t, picked_words[:], picked_scales[:], True, True)
 
         hz_picked = sb("hz_picked", [P, S], U8)
         deal_scales(ws23_deal, ws23_raw)
-        close_up_scale_rows(nc.sync, ws23_deal)
+        close_up_scale_rows(ws23_deal)
         nc.vector.tensor_copy(hz_picked[:], xs_hz[:].indirect(hz_t[:]))
-        place_scale_rows(nc.sync, hz_scales, hz_picked)
+        place_scale_rows(hz_scales, hz_picked)
         nc.vector.tensor_copy(picked_words[:], xw[:].bitcast(U32).indirect(hz_t[:]))
-        deal_words(2)
-        deal_words(1)
+        deal_words(W3)
+        deal_words(W2)
 
         first = [sb(f"first{a}", [P, PACK, w], F32) for a, (j0, w) in enumerate(Z_PARTS)]
         second = [sb(f"second{a}", [P, PACK, w], F32) for a, (j0, w) in enumerate(Z_PARTS)]
@@ -198,31 +202,40 @@ def tile_picked_mixhprodgspan_none_po_kernel(
 
         def h_products(a):
             for t in range(PACK):
-                product(h_part(a, t), 1, t, z_words[a][:], z_scales[a][:], False, a >= last - 1)
+                product(h_part(a, t), W2, t, z_words[a][:], z_scales[a][:], False, a >= last - 1)
 
         for a in range(len(Z_PARTS)):
             fetch(a)
         for a, (j0, w) in enumerate(Z_PARTS):
             for t in range(PACK):
-                product(h_part(a, t), 2, t, picked_words[:, j0 : j0 + w], hz_scales[:, j0 : j0 + w], a in (0, last), False)
-        for a in range(len(Z_PARTS)):
-            for t in range(PACK):
+                cols = slice(j0, j0 + w)
+                product(h_part(a, t), W3, t, picked_words[:, cols], hz_scales[:, cols], a in (0, last), False)
+        for t in range(PACK):
+            multiply(0, t)
+        multiply(1, 0)
+        interleave(z_packed[0], z_planes[0])
+        multiply(1, 1)
+        quantise(0)
+        h_products(0)
+        for a in range(1, len(Z_PARTS)):
+            for t in range(2 if a == 1 else 0, PACK):
                 multiply(a, t)
-            interleave(nc.vector.tensor_copy, z_packed[a], z_planes[a])
+            interleave(z_packed[a], z_planes[a])
             quantise(a)
             h_products(a)
 
-        for t in range(2):
+        for t in range(SCALAR_BANKS):
             nc.scalar.copy(h_win[t][:, :early], h_early[t][:])
         nc.scalar.copy(h_win[0][:, early:S], h_late[0][:])
         for t in range(1, PACK):
-            if t >= 2:
+            if t >= SCALAR_BANKS:
                 nc.vector.tensor_copy(h_win[t][:, :early], h_early[t][:])
             nc.vector.tensor_copy(h_win[t][:, early:S], h_late[t][:])
 
         out_rows = out_0.rearrange("(p t) j -> p t j", t=PACK)
         out_words = out_1[0].rearrange("p c r -> p (c r)").bitcast(I32)
         o_scales = sb("o_scales", [P, S], U8)
+
         def chunk_tiles(name, tail, dtype):
             return [sb(f"{name}{c}", [P] + tail(w), dtype) for c, (j0, w) in enumerate(OUT_CHUNKS)]
 
@@ -267,9 +280,8 @@ def tile_picked_mixhprodgspan_none_po_kernel(
             nc.sync.dma_start(out_words[:, j0 : j0 + w], o_words[c][:].bitcast(I32))
 
         singles, doubles = [(t, t + 1) for t in range(PACK)], [(0, 2), (2, 4)]
-        cuts = [singles, doubles, doubles, doubles]
+        cuts = [singles, doubles, doubles, doubles[:1] + singles[2:]]
         steps = [(c, slice(*cut)) for c in range(len(OUT_CHUNKS)) for cut in cuts[c]]
-        late_chunk = len(OUT_CHUNKS) - 2
         for now, before in zip(steps + [None], [None] + steps):
             closes = before is not None and before[1].stop == PACK
             if now:
@@ -279,13 +291,10 @@ def tile_picked_mixhprodgspan_none_po_kernel(
             if now:
                 pairs(pair_min, *now, ALU.min)
             if closes:
-                copy = nc.scalar.copy if before[0] == late_chunk else nc.vector.tensor_copy
-                interleave(copy, o_packed[before[0]], span[before[0]])
+                interleave(o_packed[before[0]], span[before[0]])
             if now:
                 fours(largest, pair_max, *now, ALU.max)
-            if closes and before[0] != late_chunk:
-                if now is None:
-                    planes(late_chunk)
+            if closes:
                 planes(before[0])
             if now:
                 fours(smallest, pair_min, *now, ALU.min)

from contextlib import ExitStack

import concourse.mybir as mybir

T, S, N, W = 2048, 512, 512, 2048
FLOPS = 3 * 2 * 512 * 512 * 512

F32 = mybir.dt.float32
BF16 = mybir.dt.bfloat16
I32 = mybir.dt.int32
U32 = mybir.dt.uint32
U16 = mybir.dt.uint16
U8 = mybir.dt.uint8
FP8X4 = mybir.dt.float8_e4m3fn_x4
FP4X4 = mybir.dt.float4_e2m1fn_x4
ALU = mybir.AluOpType
COPY = mybir.ActivationFunctionType.Copy

P = 128
PACK = 4
QUADS = 4
MEMBERS = 4
Z_PARTS = ((0, 256), (256, 128), (384, 128))
OUT_CHUNKS = ((0, 128), (128, 128), (256, 128), (384, 128))
H_SPARE = 32
ROW_STEP = 8
W1, W2, W3 = 0, 1, 2
SCALAR_BANKS = 2


def tile_picked_mixhprodgspan_none_po_kernel(
    tc, x_words, x_scales, w1_words, w1_scales, gn, w2_words, w2_scales, w3_words, w3_scales,
    offs, n1, n2, hz, n3, out_0, out_1, out_2,
):
    nc = tc.nc
    with ExitStack() as ctx:
        keep = ctx.enter_context(tc.tile_pool(name="keep", bufs=1))
        psum = ctx.enter_context(tc.psum_pool(name="psum", bufs=1))

        def sb(name, shape, dtype):
            return keep.tile(shape, dtype, name=name, align_bytes=64)

        def entries(lst, start, count):
            return lst[:, start // 16 : (start + count) // 16]

        def load_scale_rows(plane, rows):
            for q in range(QUADS):
                nc.sync.dma_start(
                    plane[32 * q : 32 * q + 4, :].bitcast(I32), rows[0, 4 * q : 4 * q + 4, :].bitcast(I32)
                )

        def place_scale_rows(plane, spread):
            for q in range(QUADS):
                nc.sync.dma_start(
                    plane[32 * q : 32 * q + 4, :].bitcast(I32),
                    spread[32 * q : 32 * q + 32 : ROW_STEP, :].bitcast(I32),
                )

        def spread_scale_rows(spread, rows):
            nc.sync.dma_start(spread[0:P:ROW_STEP].bitcast(I32), rows[0].bitcast(I32))

        def close_up_scale_rows(spread):
            for r in range(1, 4):
                nc.sync.dma_start(spread[r:P:32].bitcast(I32), spread[ROW_STEP * r : P : 32].bitcast(I32))

        def interleave(dst, src):
            nc.vector.tensor_copy(
                dst[:].rearrange("p (c i) t -> p c t i", i=4),
                src[:].rearrange("p t (c i) -> p c t i", i=4),
            )

        xw = sb("xw", [P, T], I32)
        xs = sb("xs", [P, T], U8)
        w1_raw = sb("w1_raw", [P, 2 * N], U8)
        w23_raw = sb("w23_raw", [P, 4 * N], U8)
        w_raw = [w1_raw[:], w23_raw[:, : 2 * N], w23_raw[:, 2 * N :]]
        xs_hz = sb("xs_hz", [P, T], U8)
        ws1_raw = w23_raw[:, 3 * N // 2 : 5 * N // 2]
        ws1_deal = sb("ws1_deal", [P, N], U8)
        ws23_raw = sb("ws23_raw", [P, 2 * N], U8)
        ws23_deal = sb("ws23_deal", [P, 2 * N], U8)
        w_deal = [sb(f"w_deal{i}", [P, 2 * N], U8) for i in range(3)]
        ws_deal = [ws1_deal[:], ws23_deal[:, :N], ws23_deal[:, N:]]
        hz_scales = sb("hz_scales", [P, S], U8)
        h_win = [sb(f"h_win{t}", [P, S + H_SPARE], F32) for t in range(PACK)]
        offs_t = keep.tile([P, S // 16], U16, name="offs_t")
        n1_t = keep.tile([P, S // 16], U16, name="n1_t")
        n2_t = keep.tile([P, S // 16], U16, name="n2_t")
        hz_t = keep.tile([P, S // 16], U16, name="hz_t")
        n3_t = keep.tile([P, W // 16], U16, name="n3_t")
        gain = sb("gain", [P, PACK], F32)

        nc.gpsimd.memset(ws1_raw.bitcast(I32), 0)
        nc.vector.memset(xs[:].bitcast(I32), 0)
        nc.gpsimd.memset(xs_hz[:].bitcast(I32), 0)
        nc.vector.memset(ws23_raw[:].bitcast(I32), 0)

        nc.sync.dma_start(offs_t[:], offs)
        nc.sync.dma_start(w_raw[W1].bitcast(I32), w1_words[0].bitcast(I32))
        load_scale_rows(ws1_raw, w1_scales)
        nc.sync.dma_start(n1_t[:], n1)
        nc.sync.dma_start(xw[:], x_words[0].rearrange("p c r -> p (c r)").bitcast(I32))
        load_scale_rows(xs, x_scales)
        spread_scale_rows(xs_hz[:], x_scales)
        spread_scale_rows(ws23_raw[:, N:], w3_scales)
        spread_scale_rows(ws23_raw[:, :N], w2_scales)
        nc.sync.dma_start(n2_t[:], n2)
        nc.sync.dma_start(hz_t[:], hz)
        nc.sync.dma_start(gain[:], gn.rearrange("(p t) o -> p (t o)", t=PACK))
        nc.sync.dma_start(n3_t[:], n3)
        nc.gpsimd.memset(hz_scales[:].bitcast(I32), 0)
        for t in range(PACK):
            nc.gpsimd.memset(h_win[t][:, S:], 0.0)

        def deal_words(i):
            nc.vector.tensor_copy(
                w_deal[i][:].rearrange("p (t m b) -> p t m b", t=PACK, b=2),
                w_raw[i].rearrange("p (m t b) -> p t m b", t=PACK, b=2),
            )

        def deal_scales(dealt, raw):
            nc.vector.tensor_copy(
                dealt[:].rearrange("p (i t m) -> p i t m", t=PACK, m=P),
                raw[:].rearrange("p (i m t) -> p i t m", t=PACK, m=P),
            )

        def product(out, i, t, words, scales, start, stop):
            nc.tensor.matmul_mx(
                out=out,
                lhsT=w_deal[i][:, 2 * P * t : 2 * P * (t + 1)].bitcast(FP4X4),
                lhsT_scale=ws_deal[i][:, P * t : P * (t + 1)],
                rhs=words.bitcast(FP8X4),
                rhs_scale=scales,
                start=start,
                stop=stop,
            )

        picked_words = sb("picked_words", [P, S], U32)
        picked_scales = sb("picked_scales", [P, S], U8)
        deal_words(W1)
        deal_scales(ws1_deal, ws1_raw)
        nc.sync.dma_start(w_raw[W3].bitcast(I32), w3_words[0].bitcast(I32))
        nc.sync.dma_start(w_raw[W2].bitcast(I32), w2_words[0].bitcast(I32))
        nc.vector.tensor_copy(picked_words[:], xw[:].bitcast(U32).indirect(offs_t[:]))
        halves = [slice(0, S // 2), slice(S // 2, S)]
        for cols in halves:
            nc.vector.tensor_copy(picked_scales[:, cols], xs[:].indirect(entries(offs_t, cols.start, S // 2)))

        y_bank = [psum.tile([P, S], F32, name=f"bank{t}") for t in range(PACK)]
        y_win = [sb(f"y_win{t}", [P, S], F32) for t in range(PACK)]
        for cols in halves:
            product(y_bank[0][:, cols], W1, 0, picked_words[:, cols], picked_scales[:, cols], True, True)
        for t in range(1, PACK):
            product(y_bank[t][:], W1, t, picked_words[:], picked_scales[:], True, True)

        hz_picked = sb("hz_picked", [P, S], U8)
        deal_scales(ws23_deal, ws23_raw)
        close_up_scale_rows(ws23_deal)
        nc.vector.tensor_copy(hz_picked[:], xs_hz[:].indirect(hz_t[:]))
        place_scale_rows(hz_scales, hz_picked)
        nc.vector.tensor_copy(picked_words[:], xw[:].bitcast(U32).indirect(hz_t[:]))
        deal_words(W3)
        deal_words(W2)

        first = [sb(f"first{a}", [P, PACK, w], F32) for a, (j0, w) in enumerate(Z_PARTS)]
        second = [sb(f"second{a}", [P, PACK, w], F32) for a, (j0, w) in enumerate(Z_PARTS)]
        z_planes = [sb(f"z_planes{a}", [P, PACK, w], BF16) for a, (j0, w) in enumerate(Z_PARTS)]
        z_packed = [sb(f"z_packed{a}", [P, w, PACK], BF16) for a, (j0, w) in enumerate(Z_PARTS)]
        z_words = [sb(f"z_words{a}", [P, w], U32) for a, (j0, w) in enumerate(Z_PARTS)]
        z_scales = [sb(f"z_scales{a}", [P, w], U8) for a, (j0, w) in enumerate(Z_PARTS)]
        last = len(Z_PARTS) - 1

        def fetch(a):
            j0, w = Z_PARTS[a]
            for t in range(PACK):
                if a == 0:
                    nc.scalar.copy(y_win[t][:], y_bank[t][:])
                nc.scalar.activation(first[a][:, t, :], y_win[t][:].indirect(entries(n1_t, j0, w)), COPY)
                looked_up = y_win[t][:].indirect(entries(n2_t, j0, w))
                if a > 0:
                    nc.scalar.activation(second[a][:, t, :], looked_up, COPY)
                else:
                    nc.vector.tensor_copy(second[a][:, t, :], looked_up)

        def multiply(a, t):
            nc.vector.scalar_tensor_tensor(
                z_planes[a][:, t, :], first[a][:, t, :], gain[:, t : t + 1], second[a][:, t, :], ALU.mult, ALU.mult
            )

        def quantise(a):
            nc.vector.quantize_mx(
                out=z_words[a][:].bitcast(FP8X4), scales=z_scales[a][:], in_=z_packed[a][:].rearrange("p w t -> p (w t)")
            )

        early = Z_PARTS[last][0]
        h_early = [psum.tile([P, early], F32, name=f"h_early{t}") for t in range(PACK)]
        h_late = [psum.tile([P, S - early], F32, name=f"bank{t}") for t in range(PACK)]

        def h_part(a, t):
            j0, w = Z_PARTS[a]
            return h_late[t][:] if a == last else h_early[t][:, j0 : j0 + w]

        def h_products(a):
            for t in range(PACK):
                product(h_part(a, t), W2, t, z_words[a][:], z_scales[a][:], False, a >= last - 1)

        for a in range(len(Z_PARTS)):
            fetch(a)
        for a, (j0, w) in enumerate(Z_PARTS):
            for t in range(PACK):
                cols = slice(j0, j0 + w)
                product(h_part(a, t), W3, t, picked_words[:, cols], hz_scales[:, cols], a in (0, last), False)
        for t in range(PACK):
            multiply(0, t)
        multiply(1, 0)
        interleave(z_packed[0], z_planes[0])
        multiply(1, 1)
        quantise(0)
        h_products(0)
        for a in range(1, len(Z_PARTS)):
            for t in range(2 if a == 1 else 0, PACK):
                multiply(a, t)
            interleave(z_packed[a], z_planes[a])
            quantise(a)
            h_products(a)

        for t in range(SCALAR_BANKS):
            nc.scalar.copy(h_win[t][:, :early], h_early[t][:])
        nc.scalar.copy(h_win[0][:, early:S], h_late[0][:])
        for t in range(1, PACK):
            if t >= SCALAR_BANKS:
                nc.vector.tensor_copy(h_win[t][:, :early], h_early[t][:])
            nc.vector.tensor_copy(h_win[t][:, early:S], h_late[t][:])

        out_rows = out_0.rearrange("(p t) j -> p t j", t=PACK)
        out_words = out_1[0].rearrange("p c r -> p (c r)").bitcast(I32)
        o_scales = sb("o_scales", [P, S], U8)

        def chunk_tiles(name, tail, dtype):
            return [sb(f"{name}{c}", [P] + tail(w), dtype) for c, (j0, w) in enumerate(OUT_CHUNKS)]

        members = chunk_tiles("members", lambda w: [PACK, w, MEMBERS], F32)
        pair_max = chunk_tiles("pair_max", lambda w: [PACK, w, 2], F32)
        pair_min = chunk_tiles("pair_min", lambda w: [PACK, w, 2], F32)
        largest = chunk_tiles("largest", lambda w: [PACK, w], F32)
        smallest = chunk_tiles("smallest", lambda w: [PACK, w], F32)
        span = chunk_tiles("span", lambda w: [PACK, w], F32)
        o_packed = chunk_tiles("o_packed", lambda w: [w, PACK], BF16)
        o_words = chunk_tiles("o_words", lambda w: [w], U32)

        for c, (j0, w) in enumerate(OUT_CHUNKS):
            for t in range(PACK):
                nc.scalar.activation(
                    members[c][:, t].rearrange("p j m -> p (j m)"),
                    h_win[t][:].indirect(entries(n3_t, MEMBERS * j0, MEMBERS * w)),
                    COPY,
                )

        def pairs(dst, c, ts, op):
            nc.vector.tensor_tensor(dst[c][:, ts], members[c][:, ts, :, 0:2], members[c][:, ts, :, 2:4], op)

        def fours(dst, src, c, ts, op):
            nc.vector.tensor_tensor(dst[c][:, ts], src[c][:, ts, :, 0], src[c][:, ts, :, 1], op)

        def combine(c, ts):
            nc.vector.scalar_tensor_tensor(
                span[c][:, ts], smallest[c][:, ts], -0.5, largest[c][:, ts], ALU.mult, ALU.add
            )
            if ts.stop == PACK:
                j0, w = OUT_CHUNKS[c]
                nc.sync.dma_start(out_rows[:, :, j0 : j0 + w], span[c][:])

        def planes(c):
            j0, w = OUT_CHUNKS[c]
            nc.vector.quantize_mx(
                out=o_words[c][:].bitcast(FP8X4),
                scales=o_scales[:, j0 : j0 + w],
                in_=o_packed[c][:].rearrange("p w t -> p (w t)"),
            )
            nc.sync.dma_start(out_words[:, j0 : j0 + w], o_words[c][:].bitcast(I32))

        singles, doubles = [(t, t + 1) for t in range(PACK)], [(0, 2), (2, 4)]
        cuts = [singles, doubles, doubles, doubles[:1] + singles[2:]]
        steps = [(c, slice(*cut)) for c in range(len(OUT_CHUNKS)) for cut in cuts[c]]
        for now, before in zip(steps + [None], [None] + steps):
            closes = before is not None and before[1].stop == PACK
            if now:
                pairs(pair_max, *now, ALU.max)
            if before:
                combine(*before)
            if now:
                pairs(pair_min, *now, ALU.min)
            if closes:
                interleave(o_packed[before[0]], span[before[0]])
            if now:
                fours(largest, pair_max, *now, ALU.max)
            if closes:
                planes(before[0])
            if now:
                fours(smallest, pair_min, *now, ALU.min)
        for q in range(QUADS):
            queue = nc.scalar if q % 2 == 0 else nc.sync
            queue.dma_start(
                out_2[0, 4 * q : 4 * q + 4, :].bitcast(I32), o_scales[32 * q : 32 * q + 4, :].bitcast(I32)
            )
